import numpy as np, ml_dtypes
CORES = [48,51,52,55]
N = 4
BF = ml_dtypes.bfloat16
V, R, C, LA, HL, RO, HM = 3584, 64, 4, 256, 128, 3, 4096
Z = V - 1
def climb(fa, v, n):
    for _ in range(n): v = fa[v]
    return v
def mates(rng, fa, dp, a, e):
    key = np.arange(V)
    for _ in range(C): key = np.where(dp[key] > e, fa[key], key)
    o = np.argsort(key[:Z], kind="stable"); ks = key[o]; lo = np.searchsorted(ks, key[a]); hi = np.searchsorted(ks, key[a], side="right")
    return o[lo + (rng.random(a.shape) * (hi - lo)).astype(np.int64)]
def levels(c, top):
    m = V - 1 - R; t = int(np.sum(c)); n = [m * int(i) // t for i in c]; n[0] = min(n[0], top * R)
    for i in range(1, C): n[i] = min(n[i], 14 * n[i - 1])
    n[C - 1] += m - sum(n)
    return n
def forest(rng, n, sp, roots, num, forced):
    kd = np.full((16, V), Z); fa = np.arange(V); dp = np.zeros(V, np.int64); up = roots; pos = 0
    for d in range(C):
        key = rng.exponential(1.0, (len(up), 16)) * np.exp2(rng.integers(-sp, sp + 1, (len(up), 1)))
        for i, (u, j) in enumerate(forced[d] if d < len(forced) else ()): key[u, j] = i - 1000.0
        o = np.argsort(key, axis=None)[:n[d]]; nodes = num[pos:pos + n[d]]; pos += n[d]; u = up[o >> 4]
        kd[o & 15, u] = nodes; fa[nodes] = u; dp[nodes] = d + 1; up = nodes
    return kd, fa, dp
def lanes(rng, fa, dp):
    a = rng.integers(0, Z, LA); b = rng.integers(0, V, LA); p = rng.integers(0, C + 1, LA)
    for e in range(C): b = np.where(p == e, mates(rng, fa, dp, a, e), b)
    return a, b
def base(rng, plan=None):
    kd = np.zeros((N, 8, 16, V), np.int64); fa = np.zeros((N, 8, V), np.int64); dp = fa.copy(); pa = np.zeros((N, 8, LA), np.int64); pb = pa.copy()
    for q in range(N):
        for g in range(8):
            c, top, sp = plan(rng, q, g) if plan else (rng.integers(2, 5, C), 8, 3)
            kd[q, g], fa[q, g], dp[q, g] = forest(rng, levels(c, top), sp, rng.permutation(R), R + rng.permutation(V - 1 - R), ())
            pa[q, g], pb[q, g] = lanes(rng, fa[q, g], dp[q, g])
    x = (rng.random((N, 8, 16, V)) * 256 * np.exp2(rng.integers(-2, 1, (N, 8, 1, V)))).astype(np.int64)
    return dict(x=x, kd=kd, fa=fa, dp=dp, pa=pa, pb=pb, w=rng.integers(0, 256, (N, 8, 16, 1)))
def pack(s):
    x = s["x"].copy(); x[..., Z] = 0; i4 = lambda v, *sh: np.ascontiguousarray(v.reshape(sh)).astype(np.int32)
    return {"xs": np.ascontiguousarray(x.reshape(N, 128, V)).astype(np.float32).astype(BF), "kd": i4(s["kd"], N, 128, V), "fa": i4(s["fa"], N, 8, V), "dp": i4(s["dp"], N, 8, V),
            "pa": i4(s["pa"], N, 8, LA), "pb": i4(s["pb"], N, 8, LA), "wt": i4(s["w"], N, 128, 1)}
def setup_inputs(rng):
    return pack(base(rng))
def setup_inputs_spread(rng):
    s = base(rng, lambda r, q, g: (r.integers(2, 5, C), 8, 6))
    s["x"] = (rng.random((N, 8, 16, V)) * np.exp2(rng.integers(0, 9, (N, 8, 1, V)))).astype(np.int64)
    s["w"] = (rng.random((N, 8, 16, 1)) * np.exp2(rng.integers(0, 9, (N, 8, 16, 1)))).astype(np.int64)
    return pack(s)
def setup_inputs_ends(rng):
    n = [2 * R] + [(36 * V // 100 - 2 * R) // (C - 2)] * (C - 2); n.append(V - 1 - R - sum(n)); s = base(rng)
    forced = ([(0, 0), (0, 15), (1, 0)], [(0, 0), (0, 7), (0, 14), (0, 15), (1, 0), (1, 3), (1, 15)], [(i, j) for i in range(7) for j in (0, 15)])
    k = rng.random((N, 8, 1, V)); x = 255 * rng.integers(0, 2, (N, 8, 16, V)); x = np.where(k < 0.35, 255, np.where(k < 0.6, 0, x)); w = 255 * rng.integers(0, 2, (N, 8, 16, 1))
    for q in range(N):
        for g in range(8):
            num = R + rng.permutation(V - 1 - R)
            for at, v in ((0, V - 3), (1, R), (2, V - 2), (n[0] + 3, V - 4), (n[0], R + 1)):
                j = int(np.flatnonzero(num == v)[0]); num[j] = num[at]; num[at] = v
            kd, fa, dp = forest(rng, n, 3, np.concatenate([np.array([R - 1, 0]), 1 + rng.permutation(R - 2)]), num, forced)
            s["kd"][q, g], s["fa"][q, g], s["dp"][q, g] = kd, fa, dp
            mode = (7 - g + N - 1 - q) % 4; A, B = V - 3, R; y = x[q, g]; fam = []
            for v in (A, B):
                c = kd[:, v]; c = c[c != Z]; t = kd[:, c].reshape(-1); fam.append((c, t[t != Z]))
            y[:, A] = 0; y[:, B] = 0
            for c, t in fam: y[:, c] = 255; y[:, t] = 255
            y[(q + g) % 16, fam[0][0]] = 254
            best = num[n[0] + 1:n[0] + 4] if (q + g) % 2 == 0 else num[n[0] + 3:n[0] + 4]
            y[:, best] = 255
            if mode == 0: w[q, g] = 255
            if mode == 1: y[:, fam[1][0]] = 0; y[:, fam[1][1]] = 0
            if mode == 2: y[:, fam[0][0]] = 0; y[:, fam[0][1]] = 0
            if mode == 3:
                o = rng.permutation(16)[:9]; y[o[:, None], fam[1][0][None]] = 0; y[o[:, None], fam[1][1][None]] = 0
            a, b = lanes(rng, fa, dp); end = rng.random(LA) < 0.72
            a = np.where(end, rng.choice(np.array([0, V - 2]), LA), a); b = np.where(end, rng.choice(np.array([0, Z]), LA), b)
            a = np.where(climb(fa, a, C) == R - 1, 0, a); a[LA - 1] = A; b[LA - 1] = B
            s["pa"][q, g], s["pb"][q, g] = a, b
    s["x"], s["w"] = x, w
    return pack(s)
def setup_inputs_corners(rng):
    def plan(r, q, g):
        return ((r.integers(2, 5, C), 8, 20), ([1] * (C - 1) + [8], 8, 3), ([8] + [1] * (C - 1), 16, 3), (r.integers(2, 5, C), 8, 0))[(q + g) % 4]
    s = base(rng, plan); k = rng.random((N, 8, 1, V)); s["x"] = np.where(k < 0.15, 255, np.where(k < 0.3, 0, s["x"]))
    for q in range(N):
        for g in range(8):
            fa, dp = s["fa"][q, g], s["dp"][q, g]; a = np.where(rng.random(LA) < 0.4, rng.choice(np.array([0, R - 1, R, V - 2]), LA), s["pa"][q, g]); t = rng.integers(0, 5, LA)
            b = np.where(t == 0, rng.choice(np.array([0, R - 1, R, V - 2, Z]), LA), np.where(t == 1, a, np.where(t == 2, fa[a], np.where(t == 3, mates(rng, fa, dp, a, 0), mates(rng, fa, dp, a, C - 2)))))
            s["pa"][q, g], s["pb"][q, g] = a, b
            u = (q + 2 * g) % 5
            if u == 0: s["w"][q, g] = 0
            if u == 1: s["w"][q, g] = 255
    return pack(s)
def setup_inputs_ties(rng):
    s = base(rng)
    for q in range(N):
        for g in range(8):
            m = rng.choice(np.array([0, 0, 0, 8, 9, 16]), V); y = 100 + (rng.permutation(16)[:, None] < m[None]).astype(np.int64); t = rng.random(V)
            if (q + g) % 3: y = np.where(t < 0.12, 0, np.where(t < 0.2, 255, y))
            s["x"][q, g] = y
    return pack(s)
def pairs(rng, s, q, g):
    left = V - 1 - R - 5 * LA; more = left // (C - 2); n = [LA, 2 * LA, 2 * LA + more] + [more] * (C - 3); n[C - 1] += V - 1 - R - sum(n)
    rows = np.argsort(rng.random((LA, 16)), axis=1)[:, :2]; slot = rng.integers(0, 16, 2 * LA); num = R + rng.permutation(V - 1 - R)
    forced = ((), [(i >> 1, int(rows[i >> 1, i & 1])) for i in range(2 * LA)], [(i, int(slot[i])) for i in range(2 * LA)])
    kd, fa, dp = forest(rng, n, 3, rng.permutation(R), num, forced)
    s["kd"][q, g], s["fa"][q, g], s["dp"][q, g] = kd, fa, dp
    at = np.zeros(V, np.int64); at[num[LA:3 * LA]] = np.arange(2 * LA); m = np.flatnonzero(dp == 3); t = at[fa[m]]
    win = rng.integers(0, 2, LA); hi = np.argsort(rng.random((16, LA)), axis=0) < rng.integers(9, 17, LA)[None]
    y = rng.integers(0, 64, (16, V)); x = s["x"][q, g]; low = np.flatnonzero((dp == 2) | (dp > 3)); x[:, low] = y[:, low]
    x[:, m] = 64 + y[:, m] + 128 * (hi[:, t >> 1] == ((t & 1) == win[t >> 1])[None]).astype(np.int64)
    o = rng.permutation(LA); flip = rng.integers(0, 2, LA)
    return num[LA + 2 * o + flip], num[LA + 2 * o + 1 - flip]
def fold(rng, s, q, g):
    roots = np.concatenate([1 + rng.permutation(R - 1), np.array([0])]); num = R + rng.permutation(V - 1 - R); rows = np.argsort(rng.random((8, 16)), axis=1)[:, :2]
    forced = ([(i >> 1, int(rows[i >> 1, i & 1])) for i in range(16)], [(i, int(rows[i >> 1, i & 1])) for i in range(16)])
    kd, fa, dp = forest(rng, levels(rng.integers(2, 5, C), 8), 3, roots, num, forced)
    s["kd"][q, g], s["fa"][q, g], s["dp"][q, g] = kd, fa, dp
    top = climb(fa, np.arange(V), C); x = s["x"][q, g]; x[:2, np.flatnonzero(top == 0)] = 0; x[2:, 0] = 100
    ln = np.concatenate([np.array([HL, LA - 1]), HL + 1 + rng.permutation(LA - HL - 2)[:6]]); off = (0, 0, 0, 0, 0, 0, -1, 1)
    for i in range(8):
        u = int(roots[i]); goal = (V + off[i] - 977 * int(ln[i])) & (HM - 1); c = kd[:, u]; c = c[c != Z]; c1, c2 = int(num[2 * i]), int(num[2 * i + 1])
        x[:, np.flatnonzero((top == u) & (dp > 0))] = 0
        x[0, c] = goal & 15; x[1, c] = goal >> 4; x[2:, c1] = 100; x[2:6, c2] = 255
        for v, val in ((c1, 200), (c2, 50)):
            t = kd[:, v]; t = t[t != Z]; x[2:, t] = val
    a, b = lanes(rng, fa, dp); apart = np.isin(top[a], np.concatenate([roots[:8], np.array([0])]))
    a = np.where(apart, roots[8 + rng.integers(0, R - 9, LA)], a); a[ln] = roots[:8]; b[ln] = Z
    s["w"][q, g] = 0; s["w"][q, g, 0] = 1; s["w"][q, g, 1] = 16
    return a, b
def setup_inputs_crowd(rng):
    s = base(rng)
    for q in range(N):
        for g in range(8):
            kd, fa = s["kd"][q, g], s["fa"][q, g]; kind = (q + g) % 7; cand = rng.permutation(np.flatnonzero(np.add.reduce((kd != Z).astype(np.int64), axis=0) >= 2))
            if kind < 2:
                P = cand[rng.integers(0, 3, LA)] if kind == 0 else cand[np.arange(LA) % len(cand)]
                o = np.argsort(rng.random((16, LA)) + 2 * (kd[:, P] == Z), axis=0); a, b = kd[o[0], P], kd[o[1], P]
            elif kind == 2:
                a = rng.integers(0, R, LA); b = rng.integers(0, R + 1, LA); b = np.where(b == R, Z, b)
            elif kind == 3:
                a = rng.integers(0, Z, LA); t = rng.integers(0, 4, LA); b = np.where(t < 2, a, np.where(t == 2, climb(fa, a, 1), climb(fa, a, 2)))
            elif kind == 4:
                a, b = pairs(rng, s, q, g)
            elif kind == 5:
                P = rng.permutation(np.unique(fa[R:Z])); P = P[np.arange(LA) % len(P)]
                a = kd[np.argmin(rng.random((16, LA)) + 2 * (kd[:, P] == Z), axis=0), P]; b = a.copy()
            else:
                a, b = fold(rng, s, q, g)
            s["pa"][q, g], s["pb"][q, g] = a, b
    return pack(s)
def check_inputs(d):
    bad = []
    for k, lo, hi in (("xs", 0, 255), ("kd", R, Z), ("fa", 0, Z), ("dp", 0, C), ("pa", 0, Z - 1), ("pb", 0, Z), ("wt", 0, 255)):
        v = np.asarray(d[k]).astype(np.float64)
        if not (np.min(v) >= lo and np.max(v) <= hi): bad.append("range of " + k)
        elif np.any(v != np.floor(v)): bad.append("whole numbers of " + k)
    if bad: return bad
    M = N * 8; f = np.asarray(d["fa"]).astype(np.int64).reshape(M, V); e = np.asarray(d["dp"]).astype(np.int64).reshape(M, V); k = np.asarray(d["kd"]).astype(np.int64).reshape(M, 16 * V)
    if np.any(np.asarray(d["xs"]).astype(np.float32)[..., Z] != 0): bad.append("last column of xs")
    own = np.concatenate([np.arange(R), np.array([Z])])
    if np.any(f[:, own] != own) or np.any(e[:, own] != 0): bad.append("roots")
    if np.any(f[:, R:Z] == Z) or np.any(e[:, R:Z] != np.take_along_axis(e, f[:, R:Z], 1) + 1): bad.append("fathers and depths")
    s = np.sort(k, axis=1)
    if np.any(s[:, :Z - R] != np.arange(R, Z)) or np.any(s[:, Z - R:] != Z): bad.append("every node a kid once")
    if np.any((k != Z) & (np.take_along_axis(f, k, 1) != np.tile(np.arange(V), 16))): bad.append("kids and fathers")
    return bad
def pick(t, ix):
    return np.take_along_axis(t, ix, 1)
def cols(t, ix):
    return np.take_along_axis(t, ix[:, None, :], 2)
def ring(x, k, p, o):
    m = k.shape[0]; K = cols(k, p)
    y = cols(x, K.reshape(m, 16 * LA)).reshape(m, 16, 16, LA)
    score = np.add.reduce(np.maximum(y - cols(x, o)[:, :, None, :], 0), axis=1)
    row = np.argmax(score, axis=1)
    lead = np.take_along_axis(K, row[:, None, :], 1)[:, 0]
    z = cols(x, cols(k, lead).reshape(m, 16 * LA)).reshape(m, 16, 16, LA)
    return K, row, lead, np.max(y, axis=2) + np.max(z, axis=2)
def reference(xs, kd, fa, dp, pa, pb, wt):
    M = N * 8; x = xs.astype(np.float32).astype(np.int32).reshape(M, 16, V); k = kd.astype(np.int64).reshape(M, 16, V); f = fa.astype(np.int64).reshape(M, V); e = dp.astype(np.int64).reshape(M, V)
    a = pa.astype(np.int64).reshape(M, LA); b = pb.astype(np.int64).reshape(M, LA); w = wt.astype(np.int64).reshape(M, 16, 1)
    lane = np.arange(LA); lower = np.tri(LA, k=-1, dtype=bool); at = np.arange(M)[:, None]
    asked = ((at // 8 + 1 + lane[None] % (N - 1)) % N) * 8 + at % 8
    for rnd in range(RO):
        for step in range(C):
            da, db, ga, gb = pick(e, a), pick(e, b), pick(f, a), pick(f, b)
            go = (da != db) | (ga != gb)
            a, b = np.where(go & (da >= db), ga, a), np.where(go & (db >= da), gb, b)
        F = pick(f, a); met = (a != b) & (F == pick(f, b))
        KA, rA, lA, UA = ring(x, k, a, b)
        KB, rB, lB, UB = ring(x, k, b, a)
        awin = met & (np.add.reduce((UA > UB).astype(np.int64), axis=1) >= 9)
        bwin = met & (np.add.reduce((UB > UA).astype(np.int64), axis=1) >= 9)
        first = ~np.any((F[:, :, None] == F[:, None, :]) & lower[None], axis=2)
        W, L = np.where(bwin, b, a), np.where(bwin, a, b); lW, lL = np.where(bwin, lB, lA), np.where(bwin, lA, lB); rW, rL = np.where(bwin, rB, rA), np.where(bwin, rA, rB)
        x2, k2, f2 = x.copy(), k.copy(), f.copy()
        m, i = np.nonzero(first & (awin | bwin))
        x2[m, :, W[m, i]] = (x[m, :, W[m, i]] + x[m, :, lW[m, i]]) >> 1
        m, i = np.nonzero(first & (awin | bwin) & (lW != Z) & (lL != Z))
        k2[m, rW[m, i], W[m, i]] = lL[m, i]; k2[m, rL[m, i], L[m, i]] = lW[m, i]
        f2[m, lW[m, i]] = L[m, i]; f2[m, lL[m, i]] = W[m, i]
        h = np.add.reduce(w * UA, axis=1) & (R - 1)
        m, i = np.nonzero(first & ~met)
        x2[m, :, a[m, i]] = (UA[m, :, i] + 2 * x[asked[m, i], :, h[m, i]]) >> 2
        kid = np.where(bwin[:, None, :], KB, KA)[:, lane & 15, lane]
        new = (np.add.reduce(w * (UA + UB), axis=1) + 977 * lane) & (HM - 1); new = np.where(new >= V, new - V, new)
        a = np.where(lW == Z, W, lW); b = np.where(lane < HL, kid, new)
        x, k, f = x2, k2, f2
    return {"yx": x.reshape(N, 128, V).astype(np.float32).astype(BF), "yf": f.reshape(N, 8, V).astype(np.float32)}

from concourse.bass import DstId, RemoteDMATransfer
from concourse.mybir import AluOpType as O, ActivationFunctionType as F

V, Z, LA, RO = 3584, 3583, 256, 3
f, b, i, u = "float32", "bfloat16", "int32", "uint16"
_S = dict(
    X=(3840, b), KD=(4096, i), FA=(7680, f), FP=(4096, f), FI0=(224, i), DI0=(224, i), DP16=(224, f), F0=(224, f), P2=(224, f),
    PP=(512, i), WI=(1, i), MASK=(512, b), SEG=(1024, b), ONES=(128, b), ONEF=(128, f), NC=(512, i), NM=(512, i),
    SREP=(2048, b), IDB=(128, b), NID=(128, b), BDT=(128, b), BD=(128, b), BD32=(128, f), BO=(8, b), PAT=(256, b), SEL8=(128, f),
    BDN=(128, f), SELR=(2048, b), WSEL=(2048, b), TG=(512, f), SN1=(512, f), SN2=(512, f), SN3=(512, f), SN4=(512, f),
    K=(512, u), KF=(512, f), XAB=(512, b), XT=(512, b), Y0=(4096, b), Y1=(4096, b), Z0=(4096, b), Z1=(4096, b), YM0=(4096, b), YM1=(4096, b),
    M1=(8192, b), M2=(8192, b), KEY=(256, f), KEYB=(256, f), OH=(256, b), PK=(256, f), TL=(256, f), SL=(256, f), K2=(512, u),
    FR=(256, f), FM=(256, f), SF=(256, f), EQD=(256, b), EQS=(1920, b), TC=(256, f), SC_=(256, f),
    KT=(256, f), KS=(256, f), XL=(512, b), VALS=(768, f), GF=(512, f), GFI=(512, i), GL=(512, b),
    LRS=(256, f), DLR=(256, f), TK=(512, f), NK=(512, f), RT=(256, f), XN=(256, i),
    RX0=(208, b), RX1=(208, b), RX2=(208, b))
_A = dict(
    WF=(1, f), PM=(2, f), PR=(2, i), PMI=(2, i), C16=(16, i), LW=(16, f), DUM4=(64, f), C977=(16, f), R3=(16, f), Q3=(16, i), T3=(16, f),
    CLI=(16, i), CL=(16, u), L0=(32, u), LAB=(32, u), LL=(32, u), LH=(16, u), LX=(16, u), LS=(16, u), LKF=(64, u),
    NXT=(48, f), FIX=(32, i), D16=(32, f), NH=(32, f), H2=(32, f), H1=(32, f), TT=(32, f), A3=(32, f), MN=(16, f), MP=(16, f), HH=(64, f), EQ=(64, f),
    DA=(64, f), DB=(64, f), PA_=(64, f), PB_=(64, f), ACC=(32, f), T0=(32, f), D0=(32, f), P0=(32, f), AR=(32, f),
    AB=(32, f), NE=(16, f), MET=(16, f), UNM=(16, f), THR=(32, f), LF=(32, f), COM=(16, f),
    LNZ=(32, f), CML=(16, f), DIF=(64, f), NA=(32, f), BASE=(40, f), DF=(40, f), CMU=(16, f), CST=(16, f),
    SI=(16, i), HF=(16, f), AW=(16, f), BW=(40, f), S1=(16, f), ACT=(16, f), SW4=(64, f), DX=(16, f), Q1=(16, f), Q2=(16, f),
    ST=(8, f), SX=(8, i), SG=(8, f))
_AT, _N = {}, {f: 0, i: 0, u: 0}
for _k, (_n, _d) in _A.items():
    _AT[_k] = ("PK" + _d, _N[_d]); _N[_d] += (_n + 15) // 16 * 16
SCRATCH = {k: ("sbuf", [128, n], d) for k, (n, d) in _S.items()}
SCRATCH.update({"PK" + d: ("sbuf", [128, n], d) for d, n in _N.items()})
SCRATCH["FD"] = ("dram", [8, 3584], f)
_P = dict(xr0=1024, xr1=1024, sc=512, oht=512, lr=512, mb=512)
SCRATCH.update({k: ("psum", [128, n], f) for k, n in _P.items()})
SEMAPHORES = ["sV", "sS", "sT", "sG", "arr0", "arr1", "arr2", "snt"] + ["d%d" % k for k in range(20)]


def rank_program(g, core, T, topo):
    rank = T.rank_of(core)
    if rank is None:
        return
    queues = {"V": g.vector, "S": g.scalar, "T": g.tensor, "G": g, "Y": g.sync}
    sems = {"V": "sV", "S": "sS", "T": "sT", "G": "sG"}
    count = {"V": 0, "S": 0, "T": 0, "G": 0}
    seen = {}
    log = {}
    dsem = [0]

    def B(name, lo=0, hi=None, step=1, rows=None):
        w = _P[name] if name in _P else (_S[name] if name in _S else _A[name])[0]
        return ("b", name, lo, w if hi is None else hi, step, rows)

    def I(win, off):
        return ("i", win, off)

    def ap(o):
        if not isinstance(o, tuple): return o
        if o[0] == "i": return ap(o[1]).indirect(ap(o[2]))
        _, n, lo, hi, st, rows = o
        if n in _AT:
            n, at = _AT[n]; lo += at; hi += at
        if rows is None: return T[n][:, lo:hi] if st == 1 else T[n][:, lo:hi:st]
        return T[n][rows, lo:hi] if st == 1 else T[n][rows, lo:hi:st]

    def spans(o):
        if not isinstance(o, tuple): return []
        if o[0] == "i": return spans(o[1]) + spans(o[2])
        return [(o[1], o[2], o[3])]

    def bank(s):
        return (s[0], s[1] // 512 * 512, (s[2] + 511) // 512 * 512)

    def wait(q, sem, val):
        if seen.get((q, sem), 0) < val:
            seen[(q, sem)] = val
            queues[q].wait_ge(T.sem[sem], val)

    def order(q, ins, outs):
        need = {}
        for spanlist, wr in ((ins, False), (outs, True)):
            for s in spanlist:
                ps = s[0] in _P
                n, lo, hi = bank(s) if ps else s
                for (l2, h2, q2, sem, val, w2) in log.get(n, ()):
                    if l2 < hi and lo < h2:
                        if q2 == q and ps and q == "T": continue
                        if wr or w2 or (ps and q2 != q):
                            need[sem] = max(need.get(sem, 0), val)
        for sem, val in need.items(): wait(q, sem, val)

    def note(q, ins, outs, sem, val):
        for spanlist, wr in ((ins, False), (outs, True)):
            for s in spanlist:
                n, lo, hi = bank(s) if s[0] in _P else s
                keep = []
                for e in log.get(n, []):
                    inside = lo <= e[0] and e[1] <= hi
                    if inside and (wr or (e[3] == sem and not e[5])): continue
                    keep.append(e)
                keep.append((lo, hi, q, sem, val, wr))
                log[n] = keep

    def do(q, out, ins, call):
        si = [s for o in ins for s in spans(o)]
        so = spans(out)
        if isinstance(out, tuple) and out[0] == "i":
            so = spans(out[1]); si = si + spans(out[2])
        order(q, si, so)
        count[q] += 1
        call(queues[q]).then_inc(T.sem[sems[q]], 1)
        note(q, si, so, sems[q], count[q])

    def tt(out, a, c, op): do("V", out, [a, c], lambda e: e.tensor_tensor(ap(out), ap(a), ap(c), op))
    def cp(out, a): do("V", out, [a], lambda e: e.tensor_copy(ap(out), ap(a)))
    def ts(out, a, s1, op0, s2=None, op1=None):
        if op1 is None: do("V", out, [a, s1], lambda e: e.tensor_scalar(ap(out), ap(a), ap(s1), None, op0))
        else: do("V", out, [a, s1, s2], lambda e: e.tensor_scalar(ap(out), ap(a), ap(s1), ap(s2), op0, op1))
    def scan(out, d0, d1, op0, op1): do("V", out, [d0, d1], lambda e: e.tensor_tensor_scan(ap(out), ap(d0), ap(d1), 0.0, op0, op1))
    def fill(out, val): do("V", out, [], lambda e: e.memset(ap(out), val))
    def act(out, a, scale=1.0): do("S", out, [a], lambda e: e.activation(ap(out), ap(a), F.Copy, scale=scale))
    def mm(out, l, r, start, stop): do("T", out, [l, r], lambda e: e.matmul(ap(out), ap(l), ap(r), start, stop))
    def iota(out, pattern, base, cm): do("G", out, [], lambda e: e.iota(ap(out), pattern, base, cm, allow_small_or_imprecise_dtypes=True))
    def asel(out, a, pattern, op, base, cm): do("G", out, [a], lambda e: e.affine_select(ap(out), ap(a), pattern, op, 0.0, base, cm))

    def func(name, at, a, fn, scale, bias):
        o = B(name, at, at + 128)
        do("S", o, [a], lambda e: e.activation(ap(o), ap(a), fn, bias=bias, scale=scale))

    def dma(q, pairs, fresh=False):
        sem = "d%d" % dsem[0]; dsem[0] += 1
        ii, oo = [], []
        for out, a in pairs:
            si, so = spans(a), spans(out)
            order(q, si, [] if fresh else so)
            queues[q].dma_start(ap(out) if isinstance(out, tuple) else out, ap(a) if isinstance(a, tuple) else a).then_inc(T.sem[sem], 16)
            ii += si; oo += so
        for s in ii: note(q + sem, [s], [], sem, 16 * len(pairs))
        for s in oo: log.setdefault(s[0], []).append((s[1], s[2], q + sem, sem, 16 * len(pairs), True))
        return sem, 16 * len(pairs)

    dma("Y", [(B("FI0"), T.fa[:, :])])
    dma("S", [(B("DI0"), T.dp[:, :])])
    dma("Y", [(B("PP", 0, 256, 1, slice(0, 8)), T.pa[:, :]), (B("PP", 256, 512, 1, slice(0, 8)), T.pb[:, :]), (B("WI"), T.wt[:, :])])
    dma("S", [(B("X", 0, V), T.xs[:, :])])

    fill(B("ONES", 0, 128), 1.0); fill(B("ONEF"), 1.0)
    iota(B("PR"), [[0, 2]], 0, 1)
    iota(B("NC"), [[1, 512]], 0, 0)
    asel(B("SEL8"), B("ONEF"), [[-1, 8], [0, 16]], O.is_equal, 0, 1)
    asel(B("BDT"), B("ONES", 0, 128), [[-16, 8], [0, 16]], O.is_ge, 0, 1)
    asel(B("BD"), B("BDT"), [[16, 8], [0, 16]], O.is_ge, 15, -1)
    iota(B("C16"), [[16, 16]], 0, 0)
    iota(B("CLI"), [[16, 16]], 15, 0)
    asel(B("IDB"), B("ONES", 0, 128), [[-1, 128]], O.is_equal, 0, 1)
    iota(B("FA", 4096, 7680), [[1, 3584]], 0, 0)
    ts(B("DP16"), B("DI0"), 1.0, O.max, 0.0625, O.mult)
    tt(B("F0"), B("DP16"), B("FI0"), O.add)
    sem, val = dma("Y", [(T.FD[:, :], B("F0"))])
    wait("Y", sem, val); wait("S", sem, val)
    dma("Y", [(B("FA", 0, V, 1, slice(r, 128, 16)), T.FD[:, :]) for r in range(0, 16, 2)])
    dma("S", [(B("FA", 0, V, 1, slice(r, 128, 16)), T.FD[:, :]) for r in range(1, 16, 2)], True)
    dma("Y", [(B("KD", 0, 1792), T.kd[:, 0:1792])])
    dma("S", [(B("KD", 1792, V), T.kd[:, 1792:V])])

    fill(B("FA", 3584, 4096), 0.0)
    ts(B("PMI"), B("PR"), 15, O.bitwise_and)
    ts(B("NM"), B("NC"), 15, O.bitwise_and)
    cp(B("PM"), B("PMI"))
    pm = B("PM", 0, 1)
    ts(B("MASK"), B("NM"), pm, O.is_equal)
    ts(B("SEG", 0, 512), B("NM"), 1.0, O.min)
    cp(B("NK", 0, 512, 1, slice(0, 8)), B("PP", 0, 512, 1, slice(0, 8)))
    mm(B("mb"), B("SEL8", 0, 128, 1, slice(0, 8)), B("NK", 0, 512, 1, slice(0, 8)), True, True)
    cp(B("WF"), B("WI"))
    tt(B("TG"), B("mb"), B("MASK"), O.mult)
    scan(B("SN1"), B("SEG", 0, 512), B("TG"), O.mult, O.add)
    cp(B("L0"), B("SN1", 15, 512, 16))
    cp(B("NXT", 16, 48), B("SN1", 15, 512, 16))
    ts(B("TL", 0, 128), B("NM", 0, 128), 1.0, O.add)
    fill(B("Z0", 0, 2048), 1.0)
    tt(B("BDN"), B("TL", 0, 128), B("BD"), O.mult)
    asel(B("SREP"), B("Z0", 0, 2048), [[1, 128], [0, 16]], O.is_equal, 0, -1)
    for r in range(16):
        func("Z1", 128 * r, B("BDN"), F.Abs, 1.0, -float(r + 1))
        func("SELR", 128 * r, B("Z1", 128 * r, 128 * r + 128), F.Relu, -1.0, 1.0)
    do("S", B("WSEL"), [B("SELR"), B("WF")], lambda e: e.activation(ap(B("WSEL")), ap(B("SELR")), F.Copy, scale=ap(B("WF"))))
    cp(B("SEG", 512, 1024), B("SEG", 0, 512))
    ts(B("PAT"), B("NM", 0, 256), -1.0, O.mult, 15.0, O.add)
    ts(B("LW"), B("C16"), pm, O.add)
    for k in range(4): ts(B("DUM4", 16 * k, 16 * k + 16), B("LW"), float(V + 256 * (k & 1)), O.add)
    ts(B("C977"), B("LW"), 977.0, O.mult)
    ts(B("Q3"), B("LW"), 1.0 / 3, O.mult, -0.333, O.add)
    ts(B("T3"), B("Q3"), -3.0, O.mult)
    tt(B("T3"), B("T3"), B("LW"), O.add)
    ts(B("R3"), B("T3"), 64.0, O.mult, -192.0, O.add)
    cp(B("CL"), B("CLI"))
    for k in range(RO): fill(B("RX%d" % k, 192, 208), 0.0)
    ts(B("NID"), B("IDB"), -1.0, O.mult)
    cp(B("BD32"), B("BD"))
    ts(B("BO"), B("BD", 0, 128, 16), 16.0, O.mult)

    PTR = B("NXT", 16, 48)
    others = [T.cores[(rank + d) % 4] for d in (1, 2, 3)]
    eng = [e for e in topo.engines(core, others[0]) if all(e in topo.engines(core, o) for o in others)][:8]

    for rd in range(RO):
        last = rd == RO - 1
        order("G", [("X", 0, 64)], [])
        ids, dsts = [], []
        for d in (1, 2, 3):
            rid, pid, _ = topo.addr(T.cores[(rank + d) % 4])
            slot = 3 - d
            ids.append(DstId(rid=rid, pnc=pid)); dsts.append(T["RX%d" % rd][:, 64 * slot:64 * slot + 64])
        g.remote_dma_fused([RemoteDMATransfer(dst_ids=ids, dma_engine_mask=sum(1 << e for e in eng), remote_sem=T.sem["arr%d" % rd],
                                              srcs=[T.X[:, 0:64]], dsts=dsts)], local_sem=T.sem.snt)
        def fetch():
            tt(B("TG"), I(B("FA"), B("L0")), B("MASK"), O.mult)
        def wrap(k):
            scan(B("SN%d" % k), B("SEG", 0, 512), B("TG"), O.mult, O.add)
        def vo(k, side=None):
            return B("SN%d" % k, 15, 512, 16) if side is None else B("SN%d" % k, 15 + 256 * side, 256 + 256 * side, 16)
        fetch(); wrap(1)
        cp(B("FIX"), vo(1))
        tt(B("D16"), vo(1), B("FIX"), O.subtract)
        tt(B("TT"), PTR, B("FIX"), O.subtract)
        ts(B("NH"), B("D16"), 3.5 / 16, O.is_le)
        ts(B("H2"), B("D16"), 2.5 / 16, O.is_le, 4096.0, O.mult)
        tt(B("TT"), B("TT"), B("NH"), O.mult)
        tt(B("T0"), B("FIX"), B("H2"), O.add)
        tt(B("T0"), B("T0"), B("TT"), O.add)
        cp(B("L0"), B("T0"))
        ts(B("H1"), B("D16"), 1.5 / 16, O.is_le, 4096.0, O.mult)
        fetch()
        tt(B("A3"), B("TT"), B("FIX"), O.add)
        tt(B("MN"), B("D16", 0, 16), B("D16", 16, 32), O.min)
        wrap(2)
        tt(B("MP"), B("NXT", 16, 32), B("NXT", 32, 48), O.min)
        tt(B("T0"), vo(2), B("H1"), O.add)
        cp(B("L0"), B("T0"))
        for e in range(1, 4): ts(B("HH", 16 * e, 16 * e + 16), B("MN"), (e + 0.5) / 16, O.is_gt)
        fetch()
        tt(B("EQ", 48, 64), B("A3", 0, 16), B("A3", 16, 32), O.is_equal)
        tt(B("DA", 48, 64), B("NXT", 16, 32), B("A3", 0, 16), O.subtract)
        tt(B("DB", 48, 64), B("NXT", 32, 48), B("A3", 16, 32), O.subtract)
        wrap(3)
        tt(B("EQ", 32, 48), vo(2, 0), vo(2, 1), O.is_equal)
        cp(B("L0"), vo(3))
        tt(B("DA", 32, 48), B("A3", 0, 16), vo(2, 0), O.subtract)
        fetch()
        tt(B("DB", 32, 48), B("A3", 16, 32), vo(2, 1), O.subtract)
        tt(B("EQ", 16, 32), vo(3, 0), vo(3, 1), O.is_equal)
        tt(B("DA", 16, 32), vo(2, 0), vo(3, 0), O.subtract)
        tt(B("DB", 16, 32), vo(2, 1), vo(3, 1), O.subtract)
        ts(B("HH", 0, 16), B("MP"), 63.5, O.is_gt)
        tt(B("EQ", 16, 64), B("EQ", 16, 64), B("HH", 16, 64), O.mult)
        wrap(4)
        tt(B("PA_", 16, 64), B("DA", 16, 64), B("EQ", 16, 64), O.mult)
        tt(B("PB_", 16, 64), B("DB", 16, 64), B("EQ", 16, 64), O.mult)
        tt(B("EQ", 0, 16), vo(4, 0), vo(4, 1), O.is_equal)
        tt(B("D0"), vo(3), vo(4), O.subtract)
        tt(B("ACC", 0, 16), B("PA_", 16, 32), B("PA_", 32, 48), O.add)
        tt(B("ACC", 16, 32), B("PB_", 16, 32), B("PB_", 32, 48), O.add)
        tt(B("HH", 0, 16), B("EQ", 0, 16), B("HH", 0, 16), O.mult)
        tt(B("AR"), B("ACC"), vo(4), O.add)
        tt(B("ACC", 0, 16), B("PA_", 48, 64), B("AR", 0, 16), O.add)
        tt(B("ACC", 16, 32), B("PB_", 48, 64), B("AR", 16, 32), O.add)
        tt(B("P0", 0, 16), B("D0", 0, 16), B("HH", 0, 16), O.mult)
        tt(B("P0", 16, 32), B("D0", 16, 32), B("HH", 0, 16), O.mult)
        tt(B("AR"), B("ACC"), B("P0"), O.add)
        cp(B("LAB"), B("AR"))
        cp(B("K", 0, 256), I(B("KD", 0, V), B("LAB", 0, 16)))
        act(B("XAB"), I(B("X", 0, V), B("LAB")))
        for s in range(2):
            for h in range(2):
                mm(B("mb", 256 * s + 128 * h, 256 * s + 128 * h + 128), B("XAB", 256 * (1 - s) + 128 * h, 256 * (1 - s) + 128 * h + 128), B("IDB"), True, True)
        def ygather(s, ch):
            act(B("Y%d" % s, 1024 * ch, 1024 * ch + 1024), I(B("X", 0, V), B("K", 256 * s + 64 * ch, 256 * s + 64 * ch + 64)))
        def zgather(s, ch):
            act(B("Z%d" % s, 1024 * ch, 1024 * ch + 1024), I(B("X", 0, V), B("K2", 256 * s + 64 * ch, 256 * s + 64 * ch + 64)))
        def xrep(s, ch, sub=False):
            for k in range(2):
                mm(B("xr%d" % (ch & 1), 512 * k, 512 * k + 512), B("XT", 256 * s + 128 * (ch >> 1), 256 * s + 128 * (ch >> 1) + 128),
                   B("SREP", 1024 * (ch & 1) + 512 * k, 1024 * (ch & 1) + 512 * k + 512), True, not sub)
                if sub: mm(B("xr%d" % (ch & 1), 512 * k, 512 * k + 512), B("NID"), B("Y%d" % s, 1024 * ch + 512 * k, 1024 * ch + 512 * k + 512), False, True)
        def ymax(s, ch):
            tt(B("YM%d" % s, 1024 * ch, 1024 * ch + 1024), B("Y%d" % s, 1024 * ch, 1024 * ch + 1024), B("xr%d" % (ch & 1)), O.max)
        def yrelu(s, ch):
            xrep(s, ch, True)
            o, a = B("YM%d" % s, 1024 * ch, 1024 * ch + 1024), B("xr%d" % (ch & 1))
            do("S", o, [a], lambda e: e.activation(ap(o), ap(a), F.Relu, scale=-1.0))
        def top(M, s, ch):
            scan(B(M, 4096 * s + 1024 * ch, 4096 * s + 1024 * ch + 1024), B("SEG"),
                 B(("Y%d" if M == "M1" else "Z%d") % s, 1024 * ch, 1024 * ch + 1024), O.mult, O.max)
        def score(s, h):
            if h == 0: mm(B("sc", 0, 256), B("ONES", 0, 128, 1, slice(0, 1)), B("PAT", 0, 256, 1, slice(0, 1)), True, False)
            for j in range(16):
                mm(B("sc", 128 * h + j, 128 * h + 128, 16), B("YM%d" % s, 2048 * h + j, 2048 * h + 2048, 16), B("BO"), False, h == 1 and j == 15)
        ygather(0, 0)
        tt(B("FM"), I(B("FA", 0, V), B("LAB", 0, 16)), B("MASK", 0, 256), O.mult)
        scan(B("SF"), B("SEG", 0, 256), B("FM"), O.mult, O.add)
        cp(B("XT", 0, 256), B("mb", 0, 256))
        cp(B("K", 256, 512), I(B("KD", 0, V), B("LAB", 16, 32)))
        xrep(0, 0); xrep(0, 1)
        cp(B("XT", 256, 512), B("mb", 256, 512))
        cp(B("AB"), B("LAB"))
        cp(B("KF", 0, 256), B("K", 0, 256))
        tt(B("NE"), B("AB", 0, 16), B("AB", 16, 32), O.not_equal)
        for ch in range(4):
            if ch < 3: ygather(0, ch + 1)
            if ch == 1: act(B("FR"), I(B("FA", 0, V), B("LAB", 0, 16)))
            ymax(0, ch)
            if ch < 2: xrep(0, ch + 2)
            if ch & 1: score(0, ch >> 1)
            if ch < 3: top("M1", 0, ch)
            if ch == 0:
                tt(B("MET"), B("EQ", 0, 16), B("NE"), O.mult)
                cp(B("KF", 256, 512), B("K", 256, 512))
                for s in range(2): ts(B("THR", 16 * s, 16 * s + 16), B("MET"), -90.0, O.mult, 99.0, O.add)
                ts(B("UNM"), B("MET"), -1.0, O.mult, 1.0, O.add)
        ygather(1, 0); ygather(1, 1)
        yrelu(1, 0)
        ygather(1, 2)

        def chain(s, f1, f2, hook):
            scan(B("KEY"), B("SEG", 0, 256), B("sc", 0, 256), O.mult, O.max)
            if s == 0: top("M1", 0, 3)
            cp(B("KEYB"), I(B("KEY"), B("CL")))
            tt(B("OH"), B("sc", 0, 256), B("KEYB"), O.is_equal)
            for h in range(2):
                mm(B("oht", 256 * s + 128 * h, 256 * s + 128 * h + 128), B("OH", 128 * h, 128 * h + 128), B("IDB"), True, True)
            for c in f1: c()
            tt(B("PK"), B("oht", 256 * s, 256 * s + 256), B("KF", 256 * s, 256 * s + 256), O.mult)
            mm(B("lr", 256 * s, 256 * s + 256), B("BD32"), B("PK"), True, True)
            hook()
            for c in f2: c()
            tt(B("TL"), B("lr", 256 * s, 256 * s + 256), B("MASK", 0, 256), O.mult)
            scan(B("SL"), B("SEG", 0, 256), B("TL"), O.mult, O.add)
            cp(B("LL", 16 * s, 16 * s + 16), B("SL", 15, 256, 16))
            cp(B("K2", 256 * s, 256 * s + 256), I(B("KD", 0, V), B("LL", 16 * s, 16 * s + 16)))

        def diag():
            tt(B("EQD"), B("FR"), B("SF"), O.is_equal)
            mm(B("mb", 0, 256), B("BD"), B("EQD"), True, False)
        def later(c):
            n = 240 - 16 * c; o = sum(240 - 16 * k for k in range(c))
            ts(B("EQS", o, o + n), B("FR", 16 * c + 16, 256), B("SF", 16 * c + 15, 16 * c + 16), O.is_equal)
            mm(B("mb", 16 * c + 16, 256), B("BD"), B("EQS", o, o + n), False, c == 14)
        def kidw(k):
            tt(B("KT", 128 * k, 128 * k + 128), B("KF", 256 * k, 256 * k + 128), B("MASK", 0, 128), O.mult)

        def hook0():
            yrelu(1, 1)
            ygather(1, 3)
        chain(0, [diag, lambda: later(0)], [lambda c=c: later(c) for c in range(1, 5)], hook0)
        if last:
            tt(B("P2"), B("P2"), B("DP16"), O.subtract)
            dma("Y", [(B("FP", 0, V, 1, slice(0, 128, 16)), B("P2"))])
        xrep(1, 2); xrep(1, 3)
        score(1, 0)
        for ch in range(4): zgather(0, ch)
        for c in range(5, 10): later(c)
        ymax(1, 2)
        for c in range(10, 15): later(c)
        ymax(1, 3)
        score(1, 1)
        def keep():
            if not last: cp(B("LRS"), B("lr", 0, 256))
        chain(1, [keep, lambda: top("M1", 1, 0)], [lambda: top("M1", 1, 1)], lambda: None)
        for ch in range(2): zgather(1, ch)
        act(B("XL"), I(B("X", 0, V), B("LL")))
        act(B("GF", 256, 512), I(B("FA", 0, V), B("LL", 0, 16)))
        act(B("GF", 0, 256), I(B("FA", 0, V), B("LL", 16, 32)))
        for ch in range(2, 4): zgather(1, ch)
        top("M1", 1, 2); top("M1", 1, 3)
        cp(B("LF"), B("LL"))
        MA1, MB1, MA2, MB2 = B("M1", 15, 4096, 16), B("M1", 4111, 8192, 16), B("M2", 15, 4096, 16), B("M2", 4111, 8192, 16)
        mm(B("xr0", 0, 512), B("IDB"), B("XAB"), True, False)
        mm(B("xr0", 0, 512), B("IDB"), B("XL"), False, True)
        mm(B("xr0", 512, 768), B("IDB"), MA1, True, False)
        mm(B("xr1", 0, 256), B("IDB"), MA1, True, False)
        mm(B("xr1", 0, 256), B("NID"), MB1, False, False)
        for r in range(16):
            mm(B("xr1", 512, 544), B("WSEL", 128 * r, 128 * r + 128), B("M1", 15 + 16 * r, 8192, 256), r == 0, False)
        for ch in range(4): top("M2", 0, ch)
        mm(B("xr0", 512, 768), B("IDB"), MA2, False, True)
        mm(B("xr1", 0, 256), B("IDB"), MA2, False, False)
        def affine(out, a, scale, bias):
            do("S", out, [a], lambda e: e.activation(ap(out), ap(a), F.Copy, bias=bias, scale=scale))
        affine(B("VALS", 256, 768), B("xr0", 0, 512), 0.5, -0.3125)
        affine(B("VALS", 0, 256), B("xr0", 512, 768), 0.25, -0.3125)
        tt(B("TC"), B("mb", 0, 256), B("MASK", 0, 256), O.mult)
        if not last:
            tt(B("DLR"), B("lr", 256, 512), B("LRS"), O.subtract)
            kidw(0); kidw(1)
            for s in range(2): tt(B("TK", 256 * s, 256 * s + 256), B("oht", 256 * s, 256 * s + 256), B("DLR"), O.mult)
            scan(B("KS"), B("SEG", 0, 256), B("KT"), O.mult, O.add)
            for s in range(2): tt(B("NK", 256 * s, 256 * s + 256), B("KF", 256 * s, 256 * s + 256), B("TK", 256 * s, 256 * s + 256), O.add if s == 0 else O.subtract)
        scan(B("SC_"), B("SEG", 0, 256), B("TC"), O.mult, O.add)
        ts(B("LNZ"), B("LF"), float(Z), O.not_equal)
        tt(B("DIF", 0, 32), B("AB"), B("DUM4", 0, 32), O.subtract)
        ts(B("COM"), B("SC_", 15, 256, 16), 1.5, O.is_le)
        tt(B("DIF", 32, 64), B("LF"), B("DUM4", 32, 64), O.subtract)
        tt(B("CML"), B("LNZ", 0, 16), B("LNZ", 16, 32), O.mult)
        tt(B("CST"), B("R3"), B("UNM"), O.mult)
        tt(B("CMU"), B("COM"), B("UNM"), O.mult)
        cp(B("BASE", 0, 16), B("AB", 0, 16))
        tt(B("CML"), B("CML"), B("COM"), O.mult)
        ts(B("CST"), B("CST"), 192.0, O.add)
        tt(B("DF", 0, 16), B("AB", 16, 32), B("AB", 0, 16), O.subtract)
        if not last:
            tt(B("NA"), B("LF"), B("AB"), O.subtract)
            cp(B("BASE", 32, 40), B("KS", 15, 128, 16))
            tt(B("NA"), B("NA"), B("LNZ"), O.mult)
            tt(B("DF", 32, 40), B("KS", 143, 256, 16), B("KS", 15, 128, 16), O.subtract)
            tt(B("NA"), B("NA"), B("AB"), O.add)
            cp(B("BASE", 16, 32), B("NA", 0, 16))
            tt(B("DF", 16, 32), B("NA", 16, 32), B("NA", 0, 16), O.subtract)
        else: cp(B("GFI"), B("GF"))
        for ch in range(4): top("M2", 1, ch)
        mm(B("xr1", 0, 256), B("NID"), MB2, False, True)
        for r in range(16):
            mm(B("xr1", 512, 544), B("WSEL", 128 * r, 128 * r + 128), B("M2", 15 + 16 * r, 8192, 256), False, r == 15)
        ts(B("GL", 0, 256), B("xr1", 0, 256), 0.0, O.is_gt)
        ts(B("GL", 256, 512), B("xr1", 0, 256), 0.0, O.is_lt)
        for r in range(16):
            mm(B("mb", 0, 32), B("SELR", 128 * r, 128 * r + 128), B("GL", r, 512, 16), r == 0, r == 15)
        cp(B("SI"), B("xr1", 512, 528))
        if not last: tt(B("ST"), B("xr1", 520, 528), B("C977", 8, 16), O.add)
        ts(B("SI"), B("SI"), 63, O.bitwise_and)
        if not last: tt(B("SX"), B("xr1", 536, 544), B("ST"), O.add)
        tt(B("HF"), B("SI"), B("UNM"), O.mult)
        if not last: ts(B("SX"), B("SX"), 4095, O.bitwise_and)
        tt(B("HF"), B("HF"), B("CST"), O.add)
        if not last: ts(B("SG"), B("SX"), float(V), O.is_ge, -float(V), O.mult)
        cp(B("LH"), B("HF"))
        wait("S", "arr%d" % rd, 3 * len(eng))
        act(B("RT"), I(B("RX%d" % rd), B("LH")), 0.5)
        if not last: tt(B("NXT", 40, 48), B("SX"), B("SG"), O.add)
        tt(B("AW"), B("mb", 0, 16), B("THR", 0, 16), O.is_ge)
        for k in range(1 if last else 3):
            n = (16, 16, 8)[k]
            tt(B("BW", 16 * k, 16 * k + n), B("mb", 16, 16 + n), B("THR", 16, 16 + n), O.is_ge)
        w, q0 = (16, 32) if last else (40, 0)
        tt(B("S1"), B("AW"), B("BW", 0, 16), O.add)
        tt(B("DF", 0, w), B("DF", 0, w), B("BW", 0, w), O.mult)
        for k in range(q0 // 16, 4): tt(B("SW4", 16 * k, 16 * k + 16), B("S1"), B("CML"), O.mult)
        tt(B("ACT"), B("S1"), B("COM"), O.mult)
        tt(B("NXT", 0, w), B("BASE", 0, w), B("DF", 0, w), O.add)
        tt(B("DIF", q0, 64), B("DIF", q0, 64), B("SW4", q0, 64), O.mult)
        ts(B("Q1"), B("AW"), 256.0, O.mult)
        ts(B("Q2"), B("BW", 0, 16), 512.0, O.mult)
        tt(B("DIF", q0, 64), B("DIF", q0, 64), B("DUM4", q0, 64), O.add)
        tt(B("ACT"), B("ACT"), B("CMU"), O.add)
        tt(B("DX"), B("NXT", 0, 16), B("DUM4", 0, 16), O.subtract)
        tt(B("Q1"), B("Q1"), B("LW"), O.add)
        cp(B("LKF", q0, 64), B("DIF", q0, 64))
        tt(B("DX"), B("DX"), B("ACT"), O.mult)
        tt(B("Q1"), B("Q1"), B("Q2"), O.add)
        if not last: cp(B("L0"), PTR)
        tt(B("DX"), B("DX"), B("DUM4", 0, 16), O.add)
        cp(B("LS"), B("Q1"))
        cp(B("LX"), B("DX"))
        if not last: cp(I(B("FA", 0, 4096), B("LKF", 32, 64)), B("GF"))
        tt(B("XN"), I(B("VALS"), B("LS")), B("RT"), O.add)
        wait("V", "snt", (rd + 1) * len(eng))
        cp(I(B("X"), B("LX")), B("XN"))
        if last: cp(I(B("FP"), B("LKF", 32, 64)), B("GFI"))
        else: cp(I(B("KD"), B("LKF", 0, 32)), B("NK"))
        if rd == RO - 2:
            dma("Y", [(B("P2"), B("FA", 0, V, 1, slice(0, 128, 16)))])
    outs = [dma("S", [(T.yx[0:64, :], B("X", 0, V, 1, slice(0, 64)))]), dma("Y", [(T.yx[64:128, :], B("X", 0, V, 1, slice(64, 128)))]),
            dma("Y", [(T.yf[:, :], B("FP", 0, V, 1, slice(0, 128, 16)))])]
    for sem, val in outs: wait("Y", sem, val)
    for q in "VSTG": wait("Y", sems[q], count[q])
